import numpy as np
import ml_dtypes


def mxq(x, axis, fmt="e4m3"):
    dtype, down = {"e4m3": (ml_dtypes.float8_e4m3fn, 7), "e5m2": (ml_dtypes.float8_e5m2, 14)}[fmt]
    v = np.moveaxis(np.asarray(x, np.float32).astype(ml_dtypes.bfloat16).astype(np.float64), axis, -1)
    blocks = v.reshape(v.shape[:-1] + (-1, 32))
    amax = np.abs(blocks).max(-1, keepdims=True)
    byte = np.maximum(np.where(amax > 0, np.frexp(amax)[1] - 1 + 127, 0) - down, 1)
    scale = np.exp2(byte - 127.0)
    codes = (blocks / scale).astype(np.float32).astype(dtype).astype(np.float64)
    return np.moveaxis((codes * scale).reshape(v.shape), -1, axis)


WIDE = False


def mx_kscale(k):
    if not WIDE:
        return np.ones(k)
    levels = np.array([10, -10, 5, -5, 0])
    if k % 512:
        return np.exp2(np.random.permutation(np.resize(levels, k // 32))).repeat(32)
    a = np.empty((k // 512, 16))
    for p in range(k // 512):
        a[p, :8] = np.random.permutation(np.resize(levels, 8))
        for g in range(8):
            far = levels[np.abs(levels - a[p, g]) >= 10]
            a[p, g + 8] = far[np.random.randint(len(far))]
    return np.exp2(a.ravel()).repeat(32)


BF16 = ml_dtypes.bfloat16


def bf(x):
    return np.asarray(x, np.float32).astype(BF16)


def f64(x):
    return np.asarray(x).astype(np.float64)


E2M1 = np.array([0.0, 0.5, 1.0, 1.5, 2.0, 3.0, 4.0, 6.0, -0.0, -0.5, -1.0, -1.5, -2.0, -3.0, -4.0, -6.0])


def pack_weight(w, fmt):
    k, n = w.shape
    w = f64(bf(w)).reshape(k // 32, 32, n)
    amax = np.abs(w).max(1)
    if fmt == "e4m3":
        byte = np.frexp(amax)[1] - 1 + 127 - 7
    else:
        mant, ex = np.frexp(amax / 6.0)
        byte = np.where(mant > 0.5, ex, ex - 1) + 127
    byte = np.clip(np.where(amax > 0, byte, 1), 1, 254)
    scaled = (w * np.exp2(127.0 - byte)[:, None, :]).reshape(k, n).astype(np.float32)
    by_word = np.ascontiguousarray(scaled.reshape(k // 512, 128, 4, n).transpose(0, 1, 3, 2))
    if fmt == "e4m3":
        words = by_word.astype(ml_dtypes.float8_e4m3fn).view(np.uint8)
    else:
        c = by_word.astype(ml_dtypes.float4_e2m1fn).view(np.uint8) & 0xF
        words = c[..., 0::2] | (c[..., 1::2] << 4)
    return np.ascontiguousarray(words), np.ascontiguousarray(byte.astype(np.uint8).reshape(k // 512, 16, n))


def unpack_weight(words, scales, fmt):
    g, p, n, _ = words.shape
    if fmt == "e4m3":
        vals = np.ascontiguousarray(words).view(ml_dtypes.float8_e4m3fn).astype(np.float64)
    else:
        nib = np.empty((g, p, n, 4), np.uint8)
        nib[..., 0::2] = words & 0xF
        nib[..., 1::2] = words >> 4
        vals = E2M1[nib]
    vals = vals * np.repeat(np.exp2(scales.astype(np.float64) - 127.0), 8, axis=1)[..., None]
    return vals.transpose(0, 1, 3, 2).reshape(g * 512, n)
def pack4(w):
    words, scales = pack_weight(w, "e2m1")
    return words.reshape(words.shape[0], 128, -1), scales


def unpack4(words, scales):
    return unpack_weight(words.reshape(words.shape[0], 128, -1, 2), scales, "e2m1")


M, K, R, N, D = 2048, 512, 1024, 1024, 512


def draw0():
    s = mx_kscale(K)
    t = mx_kscale(R)
    u = mx_kscale(M)
    x = np.random.standard_normal((M, K))
    c = np.random.standard_normal((R, K))
    width = 2 * np.sqrt(K)
    state_term = np.exp(-((x ** 2).sum(1) - K) / (2 * width))
    rule_term = np.exp(-((c ** 2).sum(1) - K) / (2 * width))
    gains = np.random.standard_normal((R, N)) / np.sqrt(R)
    residual = np.random.standard_normal((M, D)) / np.sqrt(M)
    gains_words, gains_scales = pack4(gains / t[:, None])
    return {"x": bf(x * s),
            "centres": bf(c / width / s),
            "state_term": bf(state_term * u),
            "rule_term": bf(rule_term * t),
            "gains_words": gains_words,
            "gains_scales": gains_scales,
            "residual": bf(residual / u[:, None])}


def core(x, centres, state_term, rule_term, gains_words, gains_scales, residual):
    z = mxq(f64(x), 1, "e4m3") @ mxq(f64(centres), 1, "e4m3").T
    h = np.exp(z) * f64(state_term)[:, None] * f64(rule_term)
    blend = mxq(h, 1, "e4m3") @ unpack4(gains_words, gains_scales)
    credit = mxq(h, 0, "e4m3").T @ mxq(f64(residual), 0, "e4m3")
    return blend, credit


def e4m3fn_bytes(y):
    return np.clip(np.asarray(y, np.float64), -448.0, 448.0).astype(np.float32).astype(ml_dtypes.float8_e4m3fn).view(np.uint8)


def e4m3fn_values(b):
    return np.asarray(b, np.uint8).view(ml_dtypes.float8_e4m3fn).astype(np.float64)


def setup_inputs():
    d = draw0()
    x0 = np.asarray(d['x']).astype(np.float64)
    s = (np.max(np.abs(x0), axis=(0,), keepdims=True) / 448.0).astype(np.float32)
    out = {}
    for k, v in d.items():
        if k == 'x':
            out['x_bytes'] = e4m3fn_bytes(x0 / s.astype(np.float64))
            out['x_scale'] = s
        else:
            out[k] = v
    return out


def reference(x_bytes, x_scale, centres, state_term, rule_term, gains_words, gains_scales, residual):
    return core(e4m3fn_values(x_bytes) * x_scale.astype(np.float64), centres, state_term, rule_term, gains_words, gains_scales, residual)

@@ -1,0 +1,362 @@
+from contextlib import ExitStack
+
+import concourse.mybir as mybir
+from concourse.masks import make_identity
+
+M, K, R, N, D = 2048, 512, 1024, 1024, 512
+FLOPS = 2 * M * R * K + 2 * M * R * N + 2 * M * R * D
+
+F32 = mybir.dt.float32
+BF16 = mybir.dt.bfloat16
+U32 = mybir.dt.uint32
+I32 = mybir.dt.int32
+U8 = mybir.dt.uint8
+FP8 = mybir.dt.float8_e4m3fn
+FP8X4 = mybir.dt.float8_e4m3fn_x4
+FP4X4 = mybir.dt.float4_e2m1fn_x4
+ACT = mybir.ActivationFunctionType
+MULT = mybir.AluOpType.mult
+
+P = 128
+G = M // 512
+A = R // 512
+TILES = 4 * G
+
+
+def tile_takagi_sugeno_blend_credit_s8_kernel(
+    tc, x_bytes, x_scale, centres, state_term, rule_term, gains_words, gains_scales, residual, out_0, out_1
+):
+    nc = tc.nc
+    with ExitStack() as ctx:
+        keep = ctx.enter_context(tc.tile_pool(name="keep", bufs=1))
+        work = ctx.enter_context(tc.tile_pool(name="work", bufs=2))
+        psum = ctx.enter_context(tc.psum_pool(name="psum", bufs=2))
+        ctx.enter_context(tc.manual_schedule())
+
+        x_raw = keep.tile([P, G, 4, K], U8, name="x_raw")
+        c_raw = keep.tile([P, A, 4, K], BF16, name="c_raw")
+        r_raw = keep.tile([P, G, 4, D], BF16, name="r_raw")
+        g_words = keep.tile([P, A, 2 * N], U8, name="g_words", align_bytes=64)
+        g_scales = keep.tile([P, A, N], U8, name="g_scales", align_bytes=64)
+        rule_row = keep.tile([P, R], BF16, name="rule_row")
+        x_sc = keep.tile([P, 4], F32, name="x_sc")
+        st = keep.tile([P, TILES], BF16, name="st")
+        ident = keep.tile([P, P], F32, name="ident")
+        ones = keep.tile([P, P], BF16, name="ones")
+        dummy = keep.tile([P, 1], F32, name="dummy")
+
+        x_view = x_bytes.rearrange("(g p t) k -> g p t k", p=P, t=4)
+        c_view = centres.rearrange("(a m f) k -> a m f k", m=P, f=4)
+        r_view = residual.rearrange("(g p t) d -> g p t d", p=P, t=4)
+
+        nc.vector.memset(rule_row[:], 0.0)
+        nc.vector.memset(ones[:], 1.0)
+        nc.vector.memset(dummy[:], 0.0)
+        nc.vector.memset(g_scales[:].rearrange("p a n -> p (a n)").bitcast(I32), 0)
+        make_identity(nc, ident[:])
+        nc.sync.dma_start(out=x_raw[:, 0], in_=x_view[0])
+        nc.scalar.dma_start(out=x_sc[:], in_=x_scale.rearrange("o (p t) -> p (o t)", t=4))
+        nc.scalar.dma_start(out=rule_row[0:1, :], in_=rule_term.unsqueeze(0))
+        nc.sync.dma_start(out=c_raw[:, 0], in_=c_view[0])
+        nc.scalar.dma_start(
+            out=st[:].rearrange("p (g t) -> p g t", t=4),
+            in_=state_term.rearrange("(g p t) -> p g t", p=P, t=4),
+        )
+        nc.sync.dma_start(out=c_raw[:, 1], in_=c_view[1])
+        nc.sync.dma_start(out=x_raw[:, 1], in_=x_view[1])
+        nc.sync.dma_start(
+            out=g_words[:].bitcast(I32), in_=gains_words.rearrange("a p b -> p a b").bitcast(I32)
+        )
+        gs_view = gains_scales.rearrange("a q n -> q a n").bitcast(I32)
+        for q in range(4):
+            nc.sync.dma_start(out=g_scales[32 * q : 32 * q + 4].bitcast(I32), in_=gs_view[4 * q : 4 * q + 4])
+        nc.sync.dma_start(out=x_raw[:, 2], in_=x_view[2])
+        nc.sync.dma_start(out=r_raw[:, 0], in_=r_view[0])
+        nc.sync.dma_start(out=x_raw[:, 3], in_=x_view[3])
+        for g in range(1, G):
+            nc.sync.dma_start(out=r_raw[:, g], in_=r_view[g])
+        nc.scalar.activation(dummy[:], dummy[:], ACT.Exp)
+
+        c_codes = keep.tile([P, A, 512], U32, name="c_codes", align_bytes=64)
+        c_scales = keep.tile([P, A, 512], U8, name="c_scales", align_bytes=64)
+        x_codes = keep.tile([P, G, 512], U32, name="x_codes", align_bytes=64)
+        x_scales = keep.tile([P, G, 512], U8, name="x_scales", align_bytes=64)
+        b_codes = keep.tile([P, G, R], U32, name="b_codes", align_bytes=64)
+        b_scales = keep.tile([P, G, R], U8, name="b_scales", align_bytes=64)
+        r_codes = keep.tile([P, G, D], U32, name="r_codes", align_bytes=64)
+        r_scales = keep.tile([P, G, D], U8, name="r_scales", align_bytes=64)
+        rule_b = keep.tile([P, R], BF16, name="rule_b")
+
+        def bank(shape, tag, bufs):
+            tile = psum.tile(shape, F32, name=tag, bufs=bufs)
+            return tile
+
+        def quantize(codes, scales, in_):
+            nc.vector.quantize_mx(out=codes.bitcast(FP8X4), scales=scales, in_=in_)
+
+        x_bf = {}
+        x_grouped = {}
+
+        def x_cast(g, engine, halves):
+            if g not in x_bf:
+                tile = work.tile([P, 4, K], BF16, name="x_bf")
+                x_bf[g] = tile
+            for j in halves:
+                engine.tensor_copy(
+                    out=x_bf[g][:, 2 * j : 2 * j + 2].rearrange("p t k -> p (t k)"),
+                    in_=x_raw[:, g, 2 * j : 2 * j + 2].rearrange("p t k -> p (t k)").bitcast(FP8),
+                )
+
+        def x_turn(g, j, tag, bufs):
+            tr = bank([P, 2, 2, P], tag, bufs)
+            for t in range(2):
+                words = x_bf[g][:, 2 * j + t, :].bitcast(F32)
+                for u in range(2):
+                    nc.tensor.transpose(tr[:, u, t, :], words[:, u::2], ident[:])
+            return tr
+
+        def x_scale_out(g, j, tr):
+            if g not in x_grouped:
+                tile = work.tile([P, 4, P, 4], BF16, name="x_grouped", align_bytes=64)
+                x_grouped[g] = tile
+            nc.vector.tensor_tensor(
+                out=x_grouped[g][:, 2 * j : 2 * j + 2].rearrange("p t i (u e) -> p (t i) u e", u=2),
+                in0=tr[:].rearrange("p u t i -> p (u t i)").bitcast(BF16).rearrange("p (u c e) -> p c u e", u=2, e=2),
+                in1=x_sc[:].rearrange("p (u e) -> p u e", u=2).unsqueeze(1).to_broadcast([P, 256, 2, 2]),
+                op=MULT,
+            )
+
+        def x_quant(g):
+            quantize(x_codes[:, g], x_scales[:, g], x_grouped[g][:].rearrange("p t i f -> p (t i f)"))
+
+        def c_prep(a):
+            grouped = work.tile([P, 2, P, 2, 2], F32, name="c_grouped", align_bytes=64)
+            for u in range(2):
+                tr = bank([P, 2, 2, P], "mm", 6)
+                for e in range(2):
+                    words = c_raw[:, a, 2 * u + e, :].bitcast(F32)
+                    for k in range(2):
+                        nc.tensor.transpose(tr[:, e, k, :], words[:, k::2], ident[:])
+                nc.scalar.copy(out=grouped[:, u], in_=tr[:].rearrange("p e k m -> p m e k"))
+            quantize(
+                c_codes[:, a], c_scales[:, a], grouped[:].rearrange("p u m e k -> p (u m e k)").bitcast(BF16)
+            )
+
+        z, e_sb, h_planes, h_turned, h_q = {}, {}, {}, {}, {}
+
+        def z_mm(n):
+            g, t = divmod(n, 4)
+            z[n] = []
+            for a in range(A):
+                acc = bank([P, 512], "mm", 6)
+                cols = slice(128 * t, 128 * t + 128)
+                nc.tensor.matmul_mx(
+                    out=acc[:],
+                    lhsT=x_codes[:, g, cols].bitcast(FP8X4),
+                    lhsT_scale=x_scales[:, g, cols],
+                    rhs=c_codes[:, a].bitcast(FP8X4),
+                    rhs_scale=c_scales[:, a],
+                    start=True,
+                    stop=True,
+                )
+                z[n].append(acc)
+
+        def exp(n):
+            tile = work.tile([P, R], F32, name="e_sb", bufs=3)
+            for a in range(A):
+                nc.scalar.activation(tile[:, 512 * a : 512 * a + 512], z[n][a][:], ACT.Exp)
+            e_sb[n] = tile
+
+        def strength(n):
+            g, t = divmod(n, 4)
+            if t == 0:
+                tile = work.tile([P, 4, R], BF16, name="h_planes")
+                h_planes[g] = tile
+            nc.vector.scalar_tensor_tensor(
+                out=h_planes[g][:, t, :], in0=e_sb[n][:], scalar=st[:, n : n + 1], in1=rule_b[:], op0=MULT, op1=MULT
+            )
+
+        def h_turn(n):
+            g, t = divmod(n, 4)
+            tr = bank([P, A, 2, P], "tr", 2)
+            words = h_planes[g][:, t, :].bitcast(F32)
+            for a in range(A):
+                for u in range(2):
+                    first = 256 * a + 128 * u
+                    nc.tensor.transpose(tr[:, a, u, :], words[:, first : first + 128], ident[:])
+            h_turned[n] = tr
+
+        h_words = {}
+
+        def h_copy(n):
+            tile = work.tile([P, A, P, 2], F32, name="h_words", align_bytes=64, bufs=3)
+            nc.scalar.copy(out=tile[:], in_=h_turned[n][:].rearrange("m a u p -> m a p u"))
+            h_words[n] = tile
+
+        def h_quant(n):
+            codes = work.tile([P, A * P], U32, name="h_codes", align_bytes=64, bufs=3)
+            scales = work.tile([P, A * P], U8, name="h_scales", align_bytes=64, bufs=3)
+            quantize(codes[:], scales[:], h_words[n][:].rearrange("m a p u -> m (a p u)").bitcast(BF16))
+            h_q[n] = (codes, scales)
+
+        blend = {}
+        out_view = out_0.rearrange("(g p t) n -> g t p n", p=P, t=4)
+
+        def blend_mm(n):
+            codes, scales = h_q[n]
+            blend[n] = []
+            for half in range(2):
+                acc = bank([P, 512], "mm", 6)
+                for a in range(A):
+                    cols = slice(128 * a, 128 * a + 128)
+                    nc.tensor.matmul_mx(
+                        out=acc[:],
+                        lhsT=codes[:, cols].bitcast(FP8X4),
+                        lhsT_scale=scales[:, cols],
+                        rhs=g_words[:, a, 1024 * half : 1024 * half + 1024].bitcast(FP4X4),
+                        rhs_scale=g_scales[:, a, 512 * half : 512 * half + 512],
+                        start=(a == 0),
+                        stop=(a == A - 1),
+                    )
+                blend[n].append(acc)
+
+        def blend_out(n, engines):
+            g, t = divmod(n, 4)
+            tile = work.tile([P, N], F32, name="blend_sb", bufs=4)
+            for half in range(2):
+                cols = slice(512 * half, 512 * half + 512)
+                if engines[half] == "s":
+                    nc.scalar.copy(out=tile[:, cols], in_=blend[n][half][:])
+                else:
+                    nc.vector.tensor_copy(out=tile[:, cols], in_=blend[n][half][:])
+            nc.sync.dma_start(out=out_view[g, t], in_=tile[:])
+
+        b_grouped = {}
+
+        def b_group(g, parts):
+            if g not in b_grouped:
+                tile = work.tile([P, A, 2, 2, P, 4], BF16, name="b_grouped", align_bytes=64)
+                b_grouped[g] = tile
+            for part in parts:
+                a, u = divmod(part, 2)
+                cols = slice(512 * a + 256 * u, 512 * a + 256 * u + 256)
+                nc.vector.tensor_copy(
+                    out=b_grouped[g][:, a, u],
+                    in_=h_planes[g][:, :, cols].rearrange("p t (m e) -> p e m t", e=2),
+                )
+
+        def b_quant(g):
+            quantize(b_codes[:, g], b_scales[:, g], b_grouped[g][:].rearrange("p a u e m t -> p (a u e m t)"))
+
+        r_grouped = {}
+
+        def r_group(g):
+            tile = work.tile([P, D, 4], BF16, name="r_grouped", align_bytes=64)
+            nc.gpsimd.tensor_copy(out=tile[:], in_=r_raw[:, g].rearrange("p t d -> p d t"))
+            r_grouped[g] = tile
+
+        def r_quant(g):
+            quantize(r_codes[:, g], r_scales[:, g], r_grouped[g][:].rearrange("p d t -> p (d t)"))
+
+        credit = {}
+        credit_view = out_1.rearrange("(a m f) d -> a f m d", m=P, f=4)
+
+        def credit_mm(c, groups):
+            if c not in credit:
+                credit[c] = bank([P, D], "mm", 6)
+            for g in groups:
+                cols = slice(128 * c, 128 * c + 128)
+                nc.tensor.matmul_mx(
+                    out=credit[c][:],
+                    lhsT=b_codes[:, g, cols].bitcast(FP8X4),
+                    lhsT_scale=b_scales[:, g, cols],
+                    rhs=r_codes[:, g].bitcast(FP8X4),
+                    rhs_scale=r_scales[:, g],
+                    start=(g == 0),
+                    stop=(g == G - 1),
+                )
+
+        def credit_out(c):
+            tile = work.tile([P, D], F32, name="credit_sb", bufs=4)
+            if c % 2:
+                nc.scalar.copy(out=tile[:], in_=credit[c][:])
+            else:
+                nc.vector.tensor_copy(out=tile[:], in_=credit[c][:])
+            nc.sync.dma_start(out=credit_view[c // 4, c % 4], in_=tile[:])
+
+        x_cast(0, nc.vector, [0, 1])
+        tr0 = x_turn(0, 0, "mm", 6)
+        tr1 = x_turn(0, 1, "mm", 6)
+        x_scale_out(0, 0, tr0)
+        x_scale_out(0, 1, tr1)
+        x_quant(0)
+        c_prep(0)
+        for a in range(A):
+            acc = bank([P, 512], "mm", 6)
+            nc.tensor.matmul(
+                acc[:].rearrange("p (u m e) -> p u m e", u=2, e=2),
+                lhsT=ones[:],
+                rhs=rule_row[:, 512 * a : 512 * a + 512].rearrange("k (m u e) -> k u m e", u=2, e=2),
+                start=True,
+                stop=True,
+            )
+            nc.scalar.copy(out=rule_b[:, 512 * a : 512 * a + 512], in_=acc[:])
+        c_prep(1)
+        x_cast(1, nc.gpsimd, [0, 1])
+        z_mm(0)
+
+        jobs = {
+            2: [("rq", 0)], 3: [(0, 0)], 4: [(1, 0)], 5: [(2, 0), (3, 0)], 6: [("bq", 0), ("rq", 1)],
+            7: [(0, 1)], 8: [(1, 1)], 9: [(2, 1), (3, 1)], 10: [("bq", 1), ("rq", 2)],
+            11: [(0, 2), (1, 2)], 12: [(2, 2), (3, 2)], 13: [("bq", 2), ("rq", 3)],
+            14: [(0, 3), (1, 3)], 15: [(2, 3), (3, 3), ("bq", 3)],
+        }
+        for s in range(-2, TILES + 2):
+            g, t = divmod(s, 4)
+            if 0 <= s < TILES:
+                h_turn(s)
+            nxt = g + 2 if t == 3 else g + 1
+            tr = None
+            if t in (3, 0) and s >= -1 and nxt < G:
+                tr = x_turn(nxt, 0 if t == 3 else 1, "tr", 2)
+            if s + 2 < TILES:
+                exp(s + 2)
+            if 0 <= s < TILES:
+                h_copy(s)
+            if 0 <= s + 1 < TILES:
+                strength(s + 1)
+            if tr is not None:
+                x_scale_out(nxt, 0 if t == 3 else 1, tr)
+            if t == 1 and 0 <= s and nxt < G:
+                x_quant(nxt)
+            if t == 1 and 0 <= s and g + 2 < G:
+                x_cast(g + 2, nc.gpsimd, [0, 1])
+            if t == 0 and 0 <= s < TILES:
+                r_group(g)
+            for job, of in jobs.get(s, []):
+                if job == "bq":
+                    b_quant(of)
+                elif job == "rq":
+                    r_quant(of)
+                else:
+                    b_group(of, [job])
+            if 0 <= s < TILES:
+                h_quant(s)
+            if 2 <= s:
+                blend_mm(s - 2)
+                blend_out(s - 2, "ss" if s < TILES else "sv")
+            if s + 3 < TILES:
+                z_mm(s + 3)
+            if s == TILES - 2:
+                for c in (0, 1):
+                    credit_mm(c, range(G - 1))
+            if s == TILES - 1:
+                for c in (2, 3):
+                    credit_mm(c, range(G - 1))
+            if s == TILES:
+                for c in range(4):
+                    credit_mm(c, [G - 1])
+                    credit_out(c)
+        for c in range(4, 8):
+            credit_mm(c, range(G))
+            credit_out(c)

@@ -39,7 +39,7 @@ def tile_takagi_sugeno_blend_credit_s8_kernel(
         g_words = keep.tile([P, A, 2 * N], U8, name="g_words", align_bytes=64)
         g_scales = keep.tile([P, A, N], U8, name="g_scales", align_bytes=64)
         rule_row = keep.tile([P, R], BF16, name="rule_row")
-        x_sc = keep.tile([P, 4], F32, name="x_sc")
+        x_sc = keep.tile([P, K], F32, name="x_sc")
         st = keep.tile([P, TILES], BF16, name="st")
         ident = keep.tile([P, P], F32, name="ident")
         ones = keep.tile([P, P], BF16, name="ones")
@@ -55,14 +55,15 @@ def tile_takagi_sugeno_blend_credit_s8_kernel(
         nc.vector.memset(g_scales[:].rearrange("p a n -> p (a n)").bitcast(I32), 0)
         make_identity(nc, ident[:])
         nc.sync.dma_start(out=x_raw[:, 0], in_=x_view[0])
-        nc.scalar.dma_start(out=x_sc[:], in_=x_scale.rearrange("o (p t) -> p (o t)", t=4))
+        nc.scalar.dma_start(out=x_sc[:], in_=x_scale.rearrange("o k -> (o k)").partition_broadcast(P))
         nc.scalar.dma_start(out=rule_row[0:1, :], in_=rule_term.unsqueeze(0))
-        nc.sync.dma_start(out=c_raw[:, 0], in_=c_view[0])
+        for a in range(A):
+            for u in range(2):
+                nc.sync.dma_start(out=c_raw[:, a, 2 * u : 2 * u + 2], in_=c_view[a][:, 2 * u : 2 * u + 2])
         nc.scalar.dma_start(
             out=st[:].rearrange("p (g t) -> p g t", t=4),
             in_=state_term.rearrange("(g p t) -> p g t", p=P, t=4),
         )
-        nc.sync.dma_start(out=c_raw[:, 1], in_=c_view[1])
         nc.sync.dma_start(out=x_raw[:, 1], in_=x_view[1])
         nc.sync.dma_start(
             out=g_words[:].bitcast(I32), in_=gains_words.rearrange("a p b -> p a b").bitcast(I32)
@@ -70,11 +71,11 @@ def tile_takagi_sugeno_blend_credit_s8_kernel(
         gs_view = gains_scales.rearrange("a q n -> q a n").bitcast(I32)
         for q in range(4):
             nc.sync.dma_start(out=g_scales[32 * q : 32 * q + 4].bitcast(I32), in_=gs_view[4 * q : 4 * q + 4])
-        nc.sync.dma_start(out=x_raw[:, 2], in_=x_view[2])
         nc.sync.dma_start(out=r_raw[:, 0], in_=r_view[0])
-        nc.sync.dma_start(out=x_raw[:, 3], in_=x_view[3])
-        for g in range(1, G):
-            nc.sync.dma_start(out=r_raw[:, g], in_=r_view[g])
+        for g in (2, 3):
+            nc.sync.dma_start(out=x_raw[:, g], in_=x_view[g])
+            nc.sync.dma_start(out=r_raw[:, g - 1], in_=r_view[g - 1])
+        nc.sync.dma_start(out=r_raw[:, 3], in_=r_view[3])
         nc.scalar.activation(dummy[:], dummy[:], ACT.Exp)
 
         c_codes = keep.tile([P, A, 512], U32, name="c_codes", align_bytes=64)
@@ -85,7 +86,7 @@ def tile_takagi_sugeno_blend_credit_s8_kernel(
         b_scales = keep.tile([P, G, R], U8, name="b_scales", align_bytes=64)
         r_codes = keep.tile([P, G, D], U32, name="r_codes", align_bytes=64)
         r_scales = keep.tile([P, G, D], U8, name="r_scales", align_bytes=64)
-        rule_b = keep.tile([P, R], BF16, name="rule_b")
+        rule_b = psum.tile([P, R], BF16, name="rule_b", bufs=1)
 
         def bank(shape, tag, bufs):
             tile = psum.tile(shape, F32, name=tag, bufs=bufs)
@@ -97,17 +98,16 @@ def tile_takagi_sugeno_blend_credit_s8_kernel(
         x_bf = {}
         x_grouped = {}
 
-        def x_cast(g, engine, halves):
-            if g not in x_bf:
+        def x_widen(g, j):
+            if j == 0:
                 tile = work.tile([P, 4, K], BF16, name="x_bf")
                 x_bf[g] = tile
-            for j in halves:
-                engine.tensor_copy(
-                    out=x_bf[g][:, 2 * j : 2 * j + 2].rearrange("p t k -> p (t k)"),
-                    in_=x_raw[:, g, 2 * j : 2 * j + 2].rearrange("p t k -> p (t k)").bitcast(FP8),
+            for t in (2 * j, 2 * j + 1):
+                nc.vector.tensor_tensor(
+                    out=x_bf[g][:, t], in0=x_raw[:, g, t].bitcast(FP8), in1=x_sc[:], op=MULT
                 )
 
-        def x_turn(g, j, tag, bufs):
+        def x_turn(g, j, tag="tr", bufs=2):
             tr = bank([P, 2, 2, P], tag, bufs)
             for t in range(2):
                 words = x_bf[g][:, 2 * j + t, :].bitcast(F32)
@@ -115,31 +115,44 @@ def tile_takagi_sugeno_blend_credit_s8_kernel(
                     nc.tensor.transpose(tr[:, u, t, :], words[:, u::2], ident[:])
             return tr
 
-        def x_scale_out(g, j, tr):
-            if g not in x_grouped:
-                tile = work.tile([P, 4, P, 4], BF16, name="x_grouped", align_bytes=64)
+        def x_copy(g, j, tr):
+            if j == 0:
+                tile = work.tile([P, 4, P, 2], F32, name="x_grouped", align_bytes=64)
                 x_grouped[g] = tile
-            nc.vector.tensor_tensor(
-                out=x_grouped[g][:, 2 * j : 2 * j + 2].rearrange("p t i (u e) -> p (t i) u e", u=2),
-                in0=tr[:].rearrange("p u t i -> p (u t i)").bitcast(BF16).rearrange("p (u c e) -> p c u e", u=2, e=2),
-                in1=x_sc[:].rearrange("p (u e) -> p u e", u=2).unsqueeze(1).to_broadcast([P, 256, 2, 2]),
-                op=MULT,
-            )
+            nc.scalar.copy(out=x_grouped[g][:, 2 * j : 2 * j + 2], in_=tr[:].rearrange("p u t i -> p t i u"))
 
-        def x_quant(g):
-            quantize(x_codes[:, g], x_scales[:, g], x_grouped[g][:].rearrange("p t i f -> p (t i f)"))
+        def x_quant(g, pairs=((0, 1),)):
+            for first, count in pairs:
+                tiles = slice(2 * first, 2 * first + 2 * count)
+                cols = slice(256 * first, 256 * first + 256 * count)
+                quantize(
+                    x_codes[:, g, cols],
+                    x_scales[:, g, cols],
+                    x_grouped[g][:, tiles].rearrange("p t i u -> p (t i u)").bitcast(BF16),
+                )
 
-        def c_prep(a):
-            grouped = work.tile([P, 2, P, 2, 2], F32, name="c_grouped", align_bytes=64)
-            for u in range(2):
-                tr = bank([P, 2, 2, P], "mm", 6)
-                for e in range(2):
-                    words = c_raw[:, a, 2 * u + e, :].bitcast(F32)
-                    for k in range(2):
-                        nc.tensor.transpose(tr[:, e, k, :], words[:, k::2], ident[:])
-                nc.scalar.copy(out=grouped[:, u], in_=tr[:].rearrange("p e k m -> p m e k"))
+        c_grouped = {}
+
+        def c_turn(a, u):
+            tr = bank([P, 2, 2, P], "mm", 4)
+            for e in range(2):
+                words = c_raw[:, a, 2 * u + e, :].bitcast(F32)
+                for k in range(2):
+                    nc.tensor.transpose(tr[:, e, k, :], words[:, k::2], ident[:])
+            return tr
+
+        def c_copy(a, u, tr, copy):
+            if a not in c_grouped:
+                tile = work.tile([P, 2, P, 2, 2], F32, name="c_grouped", align_bytes=64)
+                c_grouped[a] = tile
+            copy(out=c_grouped[a][:, u], in_=tr[:].rearrange("p e k m -> p m e k"))
+
+        def c_quant(a, u):
+            cols = slice(256 * u, 256 * u + 256)
             quantize(
-                c_codes[:, a], c_scales[:, a], grouped[:].rearrange("p u m e k -> p (u m e k)").bitcast(BF16)
+                c_codes[:, a, cols],
+                c_scales[:, a, cols],
+                c_grouped[a][:, u].rearrange("p m e k -> p (m e k)").bitcast(BF16),
             )
 
         z, e_sb, h_planes, h_turned, h_q = {}, {}, {}, {}, {}
@@ -148,7 +161,7 @@ def tile_takagi_sugeno_blend_credit_s8_kernel(
             g, t = divmod(n, 4)
             z[n] = []
             for a in range(A):
-                acc = bank([P, 512], "mm", 6)
+                acc = bank([P, 512], "mm", 4)
                 cols = slice(128 * t, 128 * t + 128)
                 nc.tensor.matmul_mx(
                     out=acc[:],
@@ -206,7 +219,7 @@ def tile_takagi_sugeno_blend_credit_s8_kernel(
             codes, scales = h_q[n]
             blend[n] = []
             for half in range(2):
-                acc = bank([P, 512], "mm", 6)
+                acc = bank([P, 512], "mm", 4)
                 for a in range(A):
                     cols = slice(128 * a, 128 * a + 128)
                     nc.tensor.matmul_mx(
@@ -233,27 +246,32 @@ def tile_takagi_sugeno_blend_credit_s8_kernel(
 
         b_grouped = {}
 
-        def b_group(g, parts):
+        def b_group(g, parts, copy):
             if g not in b_grouped:
                 tile = work.tile([P, A, 2, 2, P, 4], BF16, name="b_grouped", align_bytes=64)
                 b_grouped[g] = tile
             for part in parts:
                 a, u = divmod(part, 2)
                 cols = slice(512 * a + 256 * u, 512 * a + 256 * u + 256)
-                nc.vector.tensor_copy(
+                copy(
                     out=b_grouped[g][:, a, u],
                     in_=h_planes[g][:, :, cols].rearrange("p t (m e) -> p e m t", e=2),
                 )
 
-        def b_quant(g):
-            quantize(b_codes[:, g], b_scales[:, g], b_grouped[g][:].rearrange("p a u e m t -> p (a u e m t)"))
+        def b_quant(g, a):
+            cols = slice(512 * a, 512 * a + 512)
+            quantize(b_codes[:, g, cols], b_scales[:, g, cols], b_grouped[g][:, a].rearrange("p u e m t -> p (u e m t)"))
 
         r_grouped = {}
 
-        def r_group(g):
-            tile = work.tile([P, D, 4], BF16, name="r_grouped", align_bytes=64)
-            nc.gpsimd.tensor_copy(out=tile[:], in_=r_raw[:, g].rearrange("p t d -> p d t"))
-            r_grouped[g] = tile
+        def r_group(g, piece):
+            if piece == 0:
+                tile = work.tile([P, D, 4], BF16, name="r_grouped", align_bytes=64)
+                r_grouped[g] = tile
+            cols = slice(64 * piece, 64 * piece + 64)
+            nc.gpsimd.tensor_scalar(
+                out=r_grouped[g][:, cols], in0=r_raw[:, g, :, cols].rearrange("p t d -> p d t"), scalar1=1.0, scalar2=0.0, op0=MULT, op1=mybir.AluOpType.add
+            )
 
         def r_quant(g):
             quantize(r_codes[:, g], r_scales[:, g], r_grouped[g][:].rearrange("p d t -> p (d t)"))
@@ -263,7 +281,7 @@ def tile_takagi_sugeno_blend_credit_s8_kernel(
 
         def credit_mm(c, groups):
             if c not in credit:
-                credit[c] = bank([P, D], "mm", 6)
+                credit[c] = bank([P, D], *({0: ("cr", 1), 4: ("tr", 2), 5: ("tr", 2)}.get(c, ("mm", 4))))
             for g in groups:
                 cols = slice(128 * c, 128 * c + 128)
                 nc.tensor.matmul_mx(
@@ -277,86 +295,97 @@ def tile_takagi_sugeno_blend_credit_s8_kernel(
                 )
 
         def credit_out(c):
-            tile = work.tile([P, D], F32, name="credit_sb", bufs=4)
+            tile = work.tile([P, D], F32, name="credit_sb", bufs=8)
             if c % 2:
                 nc.scalar.copy(out=tile[:], in_=credit[c][:])
             else:
                 nc.vector.tensor_copy(out=tile[:], in_=credit[c][:])
             nc.sync.dma_start(out=credit_view[c // 4, c % 4], in_=tile[:])
 
-        x_cast(0, nc.vector, [0, 1])
-        tr0 = x_turn(0, 0, "mm", 6)
-        tr1 = x_turn(0, 1, "mm", 6)
-        x_scale_out(0, 0, tr0)
-        x_scale_out(0, 1, tr1)
-        x_quant(0)
-        c_prep(0)
+        vcopy, scopy = nc.vector.tensor_copy, nc.scalar.copy
+        x_widen(0, 0)
+        x_widen(0, 1)
+        for u in range(2):
+            c_copy(0, u, c_turn(0, u), scopy)
+        tr = x_turn(0, 0)
+        c_quant(0, 0)
+        c_quant(0, 1)
+        x_copy(0, 0, tr)
+        tr = x_turn(0, 1)
+        x_quant(0, ((0, 1),))
+        x_widen(1, 0)
+        for u in range(2):
+            c_copy(1, u, c_turn(1, u), scopy)
+        c_quant(1, 0)
+        c_quant(1, 1)
+        x_copy(0, 1, tr)
+        z_mm(0)
+        exp(0)
+        x_quant(0, ((1, 1),))
         for a in range(A):
-            acc = bank([P, 512], "mm", 6)
             nc.tensor.matmul(
-                acc[:].rearrange("p (u m e) -> p u m e", u=2, e=2),
+                rule_b[:, 512 * a : 512 * a + 512].rearrange("p (u m e) -> p u m e", u=2, e=2),
                 lhsT=ones[:],
                 rhs=rule_row[:, 512 * a : 512 * a + 512].rearrange("k (m u e) -> k u m e", u=2, e=2),
                 start=True,
                 stop=True,
             )
-            nc.scalar.copy(out=rule_b[:, 512 * a : 512 * a + 512], in_=acc[:])
-        c_prep(1)
-        x_cast(1, nc.gpsimd, [0, 1])
-        z_mm(0)
+        z_mm(1)
+        exp(1)
+        tr = x_turn(1, 0)
+        z_mm(2)
+        x_widen(1, 1)
+        strength(0)
+        x_copy(1, 0, tr)
 
-        jobs = {
-            2: [("rq", 0)], 3: [(0, 0)], 4: [(1, 0)], 5: [(2, 0), (3, 0)], 6: [("bq", 0), ("rq", 1)],
-            7: [(0, 1)], 8: [(1, 1)], 9: [(2, 1), (3, 1)], 10: [("bq", 1), ("rq", 2)],
-            11: [(0, 2), (1, 2)], 12: [(2, 2), (3, 2)], 13: [("bq", 2), ("rq", 3)],
-            14: [(0, 3), (1, 3)], 15: [(2, 3), (3, 3), ("bq", 3)],
-        }
-        for s in range(-2, TILES + 2):
-            g, t = divmod(s, 4)
-            if 0 <= s < TILES:
+        widen = {2: (2, 0), 3: (2, 1), 5: (3, 0), 6: (3, 1)}
+        turn = {0: (1, 1), 3: (2, 0), 4: (2, 1), 6: (3, 0), 7: (3, 1)}
+        quant = {0: 1, 4: 2, 8: 3}
+        r_groups = {s: divmod(s, 4) for s in range(16)}
+        r_quants = {4: 0, 8: 1, 12: 2, 15: 3}
+        b_vector = {3: [(0, 0), (0, 1)], 4: [(0, 2)], 5: [(0, 3)], 7: [(1, 0), (1, 1)], 8: [(1, 2)], 9: [(1, 3)], 11: [(2, 0), (2, 1)], 12: [(2, 2)],
+                    14: [(3, 0), (3, 1)], 15: [(3, 2)]}
+        b_scalar = {12: [(2, 3)], 15: [(3, 3)]}
+        b_quants = {5: [(0, 0)], 6: [(0, 1)], 9: [(1, 0)], 10: [(1, 1)], 13: [(2, 0), (2, 1)], 15: [(3, 0), (3, 1)]}
+        early = {7: [(0, 0)], 11: [(0, 1)], 14: [(0, 2), (1, 0), (1, 1), (1, 2), (2, 0), (2, 1), (2, 2)],
+                 16: [(4, 0), (4, 1), (4, 2), (5, 0), (5, 1), (5, 2)], 17: [(3, 0), (3, 1), (3, 2)]}
+        for s in range(TILES + 2):
+            if s < TILES:
                 h_turn(s)
-            nxt = g + 2 if t == 3 else g + 1
-            tr = None
-            if t in (3, 0) and s >= -1 and nxt < G:
-                tr = x_turn(nxt, 0 if t == 3 else 1, "tr", 2)
+            turned = x_turn(*turn[s]) if s in turn else None
             if s + 2 < TILES:
                 exp(s + 2)
-            if 0 <= s < TILES:
+            if s < TILES:
                 h_copy(s)
-            if 0 <= s + 1 < TILES:
+            if turned is not None:
+                x_copy(*turn[s], turned)
+            if s + 1 < TILES:
                 strength(s + 1)
-            if tr is not None:
-                x_scale_out(nxt, 0 if t == 3 else 1, tr)
-            if t == 1 and 0 <= s and nxt < G:
-                x_quant(nxt)
-            if t == 1 and 0 <= s and g + 2 < G:
-                x_cast(g + 2, nc.gpsimd, [0, 1])
-            if t == 0 and 0 <= s < TILES:
-                r_group(g)
-            for job, of in jobs.get(s, []):
-                if job == "bq":
-                    b_quant(of)
-                elif job == "rq":
-                    r_quant(of)
-                else:
-                    b_group(of, [job])
-            if 0 <= s < TILES:
-                h_quant(s)
+            if 1 <= s <= TILES:
+                h_quant(s - 1)
+            for g, part in b_scalar.get(s, []):
+                b_group(g, [part], scopy)
+            if s in quant:
+                x_quant(quant[s], ((0, 2),))
+            if s in widen:
+                x_widen(*widen[s])
+            if s in r_groups:
+                g, t = r_groups[s]
+                r_group(g, 2 * t)
+                r_group(g, 2 * t + 1)
+            for g, part in b_vector.get(s, []):
+                b_group(g, [part], vcopy)
+            for g, a in b_quants.get(s, []):
+                b_quant(g, a)
+            if s in r_quants:
+                r_quant(r_quants[s])
             if 2 <= s:
                 blend_mm(s - 2)
                 blend_out(s - 2, "ss" if s < TILES else "sv")
             if s + 3 < TILES:
                 z_mm(s + 3)
-            if s == TILES - 2:
-                for c in (0, 1):
-                    credit_mm(c, range(G - 1))
-            if s == TILES - 1:
-                for c in (2, 3):
-                    credit_mm(c, range(G - 1))
-            if s == TILES:
-                for c in range(4):
-                    credit_mm(c, [G - 1])
-                    credit_out(c)
-        for c in range(4, 8):
-            credit_mm(c, range(G))
+            for c, g in early.get(s, []):
+                credit_mm(c, [g])
+        for c in range(8):
+            credit_mm(c, [G - 1] if c < 6 else range(G))
             credit_out(c)

@@ -86,7 +86,7 @@ def tile_takagi_sugeno_blend_credit_s8_kernel(
         b_scales = keep.tile([P, G, R], U8, name="b_scales", align_bytes=64)
         r_codes = keep.tile([P, G, D], U32, name="r_codes", align_bytes=64)
         r_scales = keep.tile([P, G, D], U8, name="r_scales", align_bytes=64)
-        rule_b = psum.tile([P, R], BF16, name="rule_b", bufs=1)
+        rule_b = keep.tile([P, R], BF16, name="rule_b")
 
         def bank(shape, tag, bufs):
             tile = psum.tile(shape, F32, name=tag, bufs=bufs)
@@ -264,14 +264,12 @@ def tile_takagi_sugeno_blend_credit_s8_kernel(
 
         r_grouped = {}
 
-        def r_group(g, piece):
-            if piece == 0:
+        def r_group(g, half, copy):
+            if half == 0:
                 tile = work.tile([P, D, 4], BF16, name="r_grouped", align_bytes=64)
                 r_grouped[g] = tile
-            cols = slice(64 * piece, 64 * piece + 64)
-            nc.gpsimd.tensor_scalar(
-                out=r_grouped[g][:, cols], in0=r_raw[:, g, :, cols].rearrange("p t d -> p d t"), scalar1=1.0, scalar2=0.0, op0=MULT, op1=mybir.AluOpType.add
-            )
+            cols = slice(256 * half, 256 * half + 256)
+            copy(out=r_grouped[g][:, cols], in_=r_raw[:, g, :, cols].rearrange("p t d -> p d t"))
 
         def r_quant(g):
             quantize(r_codes[:, g], r_scales[:, g], r_grouped[g][:].rearrange("p d t -> p (d t)"))
@@ -281,7 +279,7 @@ def tile_takagi_sugeno_blend_credit_s8_kernel(
 
         def credit_mm(c, groups):
             if c not in credit:
-                credit[c] = bank([P, D], *({0: ("cr", 1), 4: ("tr", 2), 5: ("tr", 2)}.get(c, ("mm", 4))))
+                credit[c] = bank([P, D], *({0: ("cr", 2), 1: ("cr", 2), 4: ("tr", 2), 5: ("tr", 2)}.get(c, ("mm", 4))))
             for g in groups:
                 cols = slice(128 * c, 128 * c + 128)
                 nc.tensor.matmul_mx(
@@ -313,23 +311,25 @@ def tile_takagi_sugeno_blend_credit_s8_kernel(
         x_copy(0, 0, tr)
         tr = x_turn(0, 1)
         x_quant(0, ((0, 1),))
-        x_widen(1, 0)
         for u in range(2):
             c_copy(1, u, c_turn(1, u), scopy)
+        x_widen(1, 0)
+        for a, copy in ((0, vcopy), (1, scopy)):
+            acc = bank([P, 512], "cr", 2)
+            nc.tensor.matmul(
+                acc[:].rearrange("p (u m e) -> p u m e", u=2, e=2),
+                lhsT=ones[:],
+                rhs=rule_row[:, 512 * a : 512 * a + 512].rearrange("k (m u e) -> k u m e", u=2, e=2),
+                start=True,
+                stop=True,
+            )
+            copy(out=rule_b[:, 512 * a : 512 * a + 512], in_=acc[:])
         c_quant(1, 0)
         c_quant(1, 1)
         x_copy(0, 1, tr)
         z_mm(0)
         exp(0)
         x_quant(0, ((1, 1),))
-        for a in range(A):
-            nc.tensor.matmul(
-                rule_b[:, 512 * a : 512 * a + 512].rearrange("p (u m e) -> p u m e", u=2, e=2),
-                lhsT=ones[:],
-                rhs=rule_row[:, 512 * a : 512 * a + 512].rearrange("k (m u e) -> k u m e", u=2, e=2),
-                start=True,
-                stop=True,
-            )
         z_mm(1)
         exp(1)
         tr = x_turn(1, 0)
@@ -341,14 +341,14 @@ def tile_takagi_sugeno_blend_credit_s8_kernel(
         widen = {2: (2, 0), 3: (2, 1), 5: (3, 0), 6: (3, 1)}
         turn = {0: (1, 1), 3: (2, 0), 4: (2, 1), 6: (3, 0), 7: (3, 1)}
         quant = {0: 1, 4: 2, 8: 3}
-        r_groups = {s: divmod(s, 4) for s in range(16)}
-        r_quants = {4: 0, 8: 1, 12: 2, 15: 3}
-        b_vector = {3: [(0, 0), (0, 1)], 4: [(0, 2)], 5: [(0, 3)], 7: [(1, 0), (1, 1)], 8: [(1, 2)], 9: [(1, 3)], 11: [(2, 0), (2, 1)], 12: [(2, 2)],
-                    14: [(3, 0), (3, 1)], 15: [(3, 2)]}
-        b_scalar = {12: [(2, 3)], 15: [(3, 3)]}
+        r_groups = {1: [(0, 0), (0, 1)], 5: [(1, 0), (1, 1)], 9: [(2, 0), (2, 1)], 10: [(3, 0), (3, 1)]}
+        r_quants = {2: 0, 6: 1, 10: 2, 13: 3}
+        b_vector = {3: [(0, 0), (0, 1)], 4: [(0, 2)], 5: [(0, 3)], 7: [(1, 0), (1, 1)], 8: [(1, 2)], 9: [(1, 3)], 11: [(2, 0), (2, 1)], 12: [(2, 2), (2, 3)],
+                    14: [(3, 0), (3, 1)], 15: [(3, 2), (3, 3)]}
+        b_scalar = {}
         b_quants = {5: [(0, 0)], 6: [(0, 1)], 9: [(1, 0)], 10: [(1, 1)], 13: [(2, 0), (2, 1)], 15: [(3, 0), (3, 1)]}
-        early = {7: [(0, 0)], 11: [(0, 1)], 14: [(0, 2), (1, 0), (1, 1), (1, 2), (2, 0), (2, 1), (2, 2)],
-                 16: [(4, 0), (4, 1), (4, 2), (5, 0), (5, 1), (5, 2)], 17: [(3, 0), (3, 1), (3, 2)]}
+        early = {7: [(0, 0), (1, 0)], 11: [(0, 1), (1, 1)], 13: [(2, 0), (2, 1), (3, 0), (3, 1)], 14: [(0, 2), (1, 2), (2, 2), (3, 2)],
+                 16: [(4, 0), (4, 1), (4, 2), (5, 0), (5, 1), (5, 2)]}
         for s in range(TILES + 2):
             if s < TILES:
                 h_turn(s)
@@ -369,10 +369,8 @@ def tile_takagi_sugeno_blend_credit_s8_kernel(
                 x_quant(quant[s], ((0, 2),))
             if s in widen:
                 x_widen(*widen[s])
-            if s in r_groups:
-                g, t = r_groups[s]
-                r_group(g, 2 * t)
-                r_group(g, 2 * t + 1)
+            for g, half in r_groups.get(s, []):
+                r_group(g, half, scopy if half else vcopy)
             for g, part in b_vector.get(s, []):
                 b_group(g, [part], vcopy)
             for g, a in b_quants.get(s, []):

@@ -39,7 +39,8 @@ def tile_takagi_sugeno_blend_credit_s8_kernel(
         g_words = keep.tile([P, A, 2 * N], U8, name="g_words", align_bytes=64)
         g_scales = keep.tile([P, A, N], U8, name="g_scales", align_bytes=64)
         rule_row = keep.tile([P, R], BF16, name="rule_row")
-        x_sc = keep.tile([P, K], F32, name="x_sc")
+        x_col = keep.tile([P, 4], F32, name="x_col")
+        x_sc = keep.tile([P, P, 4], F32, name="x_sc")
         st = keep.tile([P, TILES], BF16, name="st")
         ident = keep.tile([P, P], F32, name="ident")
         ones = keep.tile([P, P], BF16, name="ones")
@@ -54,12 +55,13 @@ def tile_takagi_sugeno_blend_credit_s8_kernel(
         nc.vector.memset(dummy[:], 0.0)
         nc.vector.memset(g_scales[:].rearrange("p a n -> p (a n)").bitcast(I32), 0)
         make_identity(nc, ident[:])
-        nc.sync.dma_start(out=x_raw[:, 0], in_=x_view[0])
-        nc.scalar.dma_start(out=x_sc[:], in_=x_scale.rearrange("o k -> (o k)").partition_broadcast(P))
+        nc.scalar.dma_start(out=x_col[:], in_=x_scale.rearrange("o (p f) -> p (o f)", f=4))
         nc.scalar.dma_start(out=rule_row[0:1, :], in_=rule_term.unsqueeze(0))
         for a in range(A):
             for u in range(2):
                 nc.sync.dma_start(out=c_raw[:, a, 2 * u : 2 * u + 2], in_=c_view[a][:, 2 * u : 2 * u + 2])
+                if a == 0 and u == 0:
+                    nc.sync.dma_start(out=x_raw[:, 0], in_=x_view[0])
         nc.scalar.dma_start(
             out=st[:].rearrange("p (g t) -> p g t", t=4),
             in_=state_term.rearrange("(g p t) -> p g t", p=P, t=4),
@@ -104,7 +106,7 @@ def tile_takagi_sugeno_blend_credit_s8_kernel(
                 x_bf[g] = tile
             for t in (2 * j, 2 * j + 1):
                 nc.vector.tensor_tensor(
-                    out=x_bf[g][:, t], in0=x_raw[:, g, t].bitcast(FP8), in1=x_sc[:], op=MULT
+                    out=x_bf[g][:, t], in0=x_raw[:, g, t].bitcast(FP8), in1=x_sc[:].rearrange("p m f -> p (m f)"), op=MULT
                 )
 
         def x_turn(g, j, tag="tr", bufs=2):
@@ -253,10 +255,11 @@ def tile_takagi_sugeno_blend_credit_s8_kernel(
             for part in parts:
                 a, u = divmod(part, 2)
                 cols = slice(512 * a + 256 * u, 512 * a + 256 * u + 256)
-                copy(
-                    out=b_grouped[g][:, a, u],
-                    in_=h_planes[g][:, :, cols].rearrange("p t (m e) -> p e m t", e=2),
-                )
+                for e in range(2):
+                    copy(
+                        out=b_grouped[g][:, a, u, e].rearrange("p (c i) t -> p c t i", i=4),
+                        in_=h_planes[g][:, :, cols].rearrange("p t (c i e) -> p e c t i", i=4, e=2)[:, e],
+                    )
 
         def b_quant(g, a):
             cols = slice(512 * a, 512 * a + 512)
@@ -265,11 +268,14 @@ def tile_takagi_sugeno_blend_credit_s8_kernel(
         r_grouped = {}
 
         def r_group(g, half, copy):
-            if half == 0:
+            if g not in r_grouped:
                 tile = work.tile([P, D, 4], BF16, name="r_grouped", align_bytes=64)
                 r_grouped[g] = tile
             cols = slice(256 * half, 256 * half + 256)
-            copy(out=r_grouped[g][:, cols], in_=r_raw[:, g, :, cols].rearrange("p t d -> p d t"))
+            copy(
+                out=r_grouped[g][:, cols].rearrange("p (c i) t -> p c t i", i=4),
+                in_=r_raw[:, g, :, cols].rearrange("p t (c i) -> p c t i", i=4),
+            )
 
         def r_quant(g):
             quantize(r_codes[:, g], r_scales[:, g], r_grouped[g][:].rearrange("p d t -> p (d t)"))
@@ -301,6 +307,10 @@ def tile_takagi_sugeno_blend_credit_s8_kernel(
             nc.sync.dma_start(out=credit_view[c // 4, c % 4], in_=tile[:])
 
         vcopy, scopy = nc.vector.tensor_copy, nc.scalar.copy
+        tr = bank([P, 4, P], "cr", 2)
+        for f in range(4):
+            nc.tensor.transpose(tr[:, f], x_col[:, f : f + 1].to_broadcast([P, P]), ident[:])
+        scopy(out=x_sc[:], in_=tr[:].rearrange("p f m -> p m f"))
         x_widen(0, 0)
         x_widen(0, 1)
         for u in range(2):
@@ -340,28 +350,23 @@ def tile_takagi_sugeno_blend_credit_s8_kernel(
 
         widen = {2: (2, 0), 3: (2, 1), 5: (3, 0), 6: (3, 1)}
         turn = {0: (1, 1), 3: (2, 0), 4: (2, 1), 6: (3, 0), 7: (3, 1)}
-        quant = {0: 1, 4: 2, 8: 3}
-        r_groups = {1: [(0, 0), (0, 1)], 5: [(1, 0), (1, 1)], 9: [(2, 0), (2, 1)], 10: [(3, 0), (3, 1)]}
-        r_quants = {2: 0, 6: 1, 10: 2, 13: 3}
-        b_vector = {3: [(0, 0), (0, 1)], 4: [(0, 2)], 5: [(0, 3)], 7: [(1, 0), (1, 1)], 8: [(1, 2)], 9: [(1, 3)], 11: [(2, 0), (2, 1)], 12: [(2, 2), (2, 3)],
-                    14: [(3, 0), (3, 1)], 15: [(3, 2), (3, 3)]}
+        quant = {1: 1, 5: 2, 8: 3}
+        r_groups = {1: [(0, 0), (0, 1)], 9: [(1, 0), (1, 1)]}
+        r_quants = {2: 0, 10: 1}
+        b_vector = {3: [(0, 0), (0, 1)], 4: [(0, 2)], 5: [(0, 3)], 7: [(1, 0), (1, 1)], 8: [(1, 2)], 9: [(1, 3)], 11: [(2, 0), (2, 1)], 12: [(2, 2), (2, 3)],}
         b_scalar = {}
-        b_quants = {5: [(0, 0)], 6: [(0, 1)], 9: [(1, 0)], 10: [(1, 1)], 13: [(2, 0), (2, 1)], 15: [(3, 0), (3, 1)]}
-        early = {7: [(0, 0), (1, 0)], 11: [(0, 1), (1, 1)], 13: [(2, 0), (2, 1), (3, 0), (3, 1)], 14: [(0, 2), (1, 2), (2, 2), (3, 2)],
-                 16: [(4, 0), (4, 1), (4, 2), (5, 0), (5, 1), (5, 2)]}
-        for s in range(TILES + 2):
-            if s < TILES:
-                h_turn(s)
+        b_quants = {5: [(0, 0)], 6: [(0, 1)], 9: [(1, 0)], 10: [(1, 1)], 13: [(2, 0), (2, 1)]}
+        early = {7: [(0, 0), (1, 0)], 11: [(0, 1), (1, 1)], 13: [(2, 0), (2, 1), (3, 0), (3, 1)]}
+        for s in range(TILES - 2):
+            h_turn(s)
             turned = x_turn(*turn[s]) if s in turn else None
             if s + 2 < TILES:
                 exp(s + 2)
-            if s < TILES:
-                h_copy(s)
+            h_copy(s)
             if turned is not None:
                 x_copy(*turn[s], turned)
-            if s + 1 < TILES:
-                strength(s + 1)
-            if 1 <= s <= TILES:
+            strength(s + 1)
+            if s >= 1:
                 h_quant(s - 1)
             for g, part in b_scalar.get(s, []):
                 b_group(g, [part], scopy)
@@ -379,11 +384,50 @@ def tile_takagi_sugeno_blend_credit_s8_kernel(
                 r_quant(r_quants[s])
             if 2 <= s:
                 blend_mm(s - 2)
-                blend_out(s - 2, "ss" if s < TILES else "sv")
+                blend_out(s - 2, "ss")
             if s + 3 < TILES:
                 z_mm(s + 3)
             for c, g in early.get(s, []):
                 credit_mm(c, [g])
-        for c in range(8):
-            credit_mm(c, [G - 1] if c < 6 else range(G))
+        n = TILES - 2
+        h_turn(n)
+        h_copy(n)
+        strength(n + 1)
+        h_quant(n - 1)
+        blend_mm(n - 2)
+        blend_out(n - 2, "ss")
+        h_turn(n + 1)
+        r_group(2, 0, vcopy)
+        h_copy(n + 1)
+        r_group(2, 1, scopy)
+        h_quant(n)
+        b_group(3, [0, 1], vcopy)
+        r_quant(2)
+        blend_mm(n - 1)
+        blend_out(n - 1, "ss")
+        h_quant(n + 1)
+        for c in (4, 5):
+            credit_mm(c, range(2))
+        b_group(3, [2, 3], vcopy)
+        r_group(3, 1, scopy)
+        r_group(3, 0, vcopy)
+        blend_mm(n)
+        blend_out(n, "ss")
+        b_quant(3, 0)
+        r_quant(3)
+        b_quant(3, 1)
+        for c in range(6):
+            credit_mm(c, [2])
+        blend_mm(n + 1)
+        blend_out(n + 1, "sv")
+        for c in range(6):
+            credit_mm(c, [3])
             credit_out(c)
+        credit_mm(6, range(4))
+        credit_out(6)
+        credit_mm(7, range(4))
+        for half, copy in ((0, scopy), (1, vcopy)):
+            cols = slice(256 * half, 256 * half + 256)
+            tile = work.tile([P, 256], F32, name="credit_half", bufs=2)
+            copy(out=tile[:], in_=credit[7][:, cols])
+            nc.sync.dma_start(out=credit_view[1, 3][:, cols], in_=tile[:])

from contextlib import ExitStack

import concourse.mybir as mybir
from concourse.masks import make_identity

M, K, R, N, D = 2048, 512, 1024, 1024, 512
FLOPS = 2 * M * R * K + 2 * M * R * N + 2 * M * R * D

F32 = mybir.dt.float32
BF16 = mybir.dt.bfloat16
U32 = mybir.dt.uint32
I32 = mybir.dt.int32
U8 = mybir.dt.uint8
FP8 = mybir.dt.float8_e4m3fn
FP8X4 = mybir.dt.float8_e4m3fn_x4
FP4X4 = mybir.dt.float4_e2m1fn_x4
ACT = mybir.ActivationFunctionType
MULT = mybir.AluOpType.mult

P = 128
G = M // 512
A = R // 512
TILES = 4 * G


def tile_takagi_sugeno_blend_credit_s8_kernel(
    tc, x_bytes, x_scale, centres, state_term, rule_term, gains_words, gains_scales, residual, out_0, out_1
):
    nc = tc.nc
    with ExitStack() as ctx:
        keep = ctx.enter_context(tc.tile_pool(name="keep", bufs=1))
        work = ctx.enter_context(tc.tile_pool(name="work", bufs=2))
        psum = ctx.enter_context(tc.psum_pool(name="psum", bufs=2))
        ctx.enter_context(tc.manual_schedule())

        x_raw = keep.tile([P, G, 4, K], U8, name="x_raw")
        c_raw = keep.tile([P, A, 4, K], BF16, name="c_raw")
        r_raw = keep.tile([P, G, 4, D], BF16, name="r_raw")
        g_words = keep.tile([P, A, 2 * N], U8, name="g_words", align_bytes=64)
        g_scales = keep.tile([P, A, N], U8, name="g_scales", align_bytes=64)
        rule_row = keep.tile([P, R], BF16, name="rule_row")
        x_col = keep.tile([P, 4], F32, name="x_col")
        x_sc = keep.tile([P, P, 4], F32, name="x_sc")
        st = keep.tile([P, TILES], BF16, name="st")
        ident = keep.tile([P, P], F32, name="ident")
        ones = keep.tile([P, P], BF16, name="ones")
        dummy = keep.tile([P, 1], F32, name="dummy")

        x_view = x_bytes.rearrange("(g p t) k -> g p t k", p=P, t=4)
        c_view = centres.rearrange("(a m f) k -> a m f k", m=P, f=4)
        r_view = residual.rearrange("(g p t) d -> g p t d", p=P, t=4)

        nc.vector.memset(rule_row[:], 0.0)
        nc.vector.memset(ones[:], 1.0)
        nc.vector.memset(dummy[:], 0.0)
        nc.vector.memset(g_scales[:].rearrange("p a n -> p (a n)").bitcast(I32), 0)
        make_identity(nc, ident[:])
        nc.scalar.dma_start(out=x_col[:], in_=x_scale.rearrange("o (p f) -> p (o f)", f=4))
        nc.scalar.dma_start(out=rule_row[0:1, :], in_=rule_term.unsqueeze(0))
        for a in range(A):
            for u in range(2):
                nc.sync.dma_start(out=c_raw[:, a, 2 * u : 2 * u + 2], in_=c_view[a][:, 2 * u : 2 * u + 2])
                if a == 0 and u == 0:
                    nc.sync.dma_start(out=x_raw[:, 0], in_=x_view[0])
        nc.scalar.dma_start(
            out=st[:].rearrange("p (g t) -> p g t", t=4),
            in_=state_term.rearrange("(g p t) -> p g t", p=P, t=4),
        )
        nc.sync.dma_start(out=x_raw[:, 1], in_=x_view[1])
        nc.sync.dma_start(
            out=g_words[:].bitcast(I32), in_=gains_words.rearrange("a p b -> p a b").bitcast(I32)
        )
        gs_view = gains_scales.rearrange("a q n -> q a n").bitcast(I32)
        for q in range(4):
            nc.sync.dma_start(out=g_scales[32 * q : 32 * q + 4].bitcast(I32), in_=gs_view[4 * q : 4 * q + 4])
        nc.sync.dma_start(out=r_raw[:, 0], in_=r_view[0])
        for g in (2, 3):
            nc.sync.dma_start(out=x_raw[:, g], in_=x_view[g])
            nc.sync.dma_start(out=r_raw[:, g - 1], in_=r_view[g - 1])
        nc.sync.dma_start(out=r_raw[:, 3], in_=r_view[3])
        nc.scalar.activation(dummy[:], dummy[:], ACT.Exp)

        c_codes = keep.tile([P, A, 512], U32, name="c_codes", align_bytes=64)
        c_scales = keep.tile([P, A, 512], U8, name="c_scales", align_bytes=64)
        x_codes = keep.tile([P, G, 512], U32, name="x_codes", align_bytes=64)
        x_scales = keep.tile([P, G, 512], U8, name="x_scales", align_bytes=64)
        b_codes = keep.tile([P, G, R], U32, name="b_codes", align_bytes=64)
        b_scales = keep.tile([P, G, R], U8, name="b_scales", align_bytes=64)
        r_codes = keep.tile([P, G, D], U32, name="r_codes", align_bytes=64)
        r_scales = keep.tile([P, G, D], U8, name="r_scales", align_bytes=64)
        rule_b = keep.tile([P, R], BF16, name="rule_b")

        def bank(shape, tag, bufs):
            tile = psum.tile(shape, F32, name=tag, bufs=bufs)
            return tile

        def quantize(codes, scales, in_):
            nc.vector.quantize_mx(out=codes.bitcast(FP8X4), scales=scales, in_=in_)

        x_bf = {}
        x_grouped = {}

        def x_widen(g, j):
            if j == 0:
                tile = work.tile([P, 4, K], BF16, name="x_bf")
                x_bf[g] = tile
            for t in (2 * j, 2 * j + 1):
                nc.vector.tensor_tensor(
                    out=x_bf[g][:, t], in0=x_raw[:, g, t].bitcast(FP8), in1=x_sc[:].rearrange("p m f -> p (m f)"), op=MULT
                )

        def x_turn(g, j, tag="tr", bufs=2):
            tr = bank([P, 2, 2, P], tag, bufs)
            for t in range(2):
                words = x_bf[g][:, 2 * j + t, :].bitcast(F32)
                for u in range(2):
                    nc.tensor.transpose(tr[:, u, t, :], words[:, u::2], ident[:])
            return tr

        def x_copy(g, j, tr):
            if j == 0:
                tile = work.tile([P, 4, P, 2], F32, name="x_grouped", align_bytes=64)
                x_grouped[g] = tile
            nc.scalar.copy(out=x_grouped[g][:, 2 * j : 2 * j + 2], in_=tr[:].rearrange("p u t i -> p t i u"))

        def x_quant(g, pairs=((0, 1),)):
            for first, count in pairs:
                tiles = slice(2 * first, 2 * first + 2 * count)
                cols = slice(256 * first, 256 * first + 256 * count)
                quantize(
                    x_codes[:, g, cols],
                    x_scales[:, g, cols],
                    x_grouped[g][:, tiles].rearrange("p t i u -> p (t i u)").bitcast(BF16),
                )

        c_grouped = {}

        def c_turn(a, u):
            tr = bank([P, 2, 2, P], "mm", 4)
            for e in range(2):
                words = c_raw[:, a, 2 * u + e, :].bitcast(F32)
                for k in range(2):
                    nc.tensor.transpose(tr[:, e, k, :], words[:, k::2], ident[:])
            return tr

        def c_copy(a, u, tr, copy):
            if a not in c_grouped:
                tile = work.tile([P, 2, P, 2, 2], F32, name="c_grouped", align_bytes=64)
                c_grouped[a] = tile
            copy(out=c_grouped[a][:, u], in_=tr[:].rearrange("p e k m -> p m e k"))

        def c_quant(a, u):
            cols = slice(256 * u, 256 * u + 256)
            quantize(
                c_codes[:, a, cols],
                c_scales[:, a, cols],
                c_grouped[a][:, u].rearrange("p m e k -> p (m e k)").bitcast(BF16),
            )

        z, e_sb, h_planes, h_turned, h_q = {}, {}, {}, {}, {}

        def z_mm(n):
            g, t = divmod(n, 4)
            z[n] = []
            for a in range(A):
                acc = bank([P, 512], "mm", 4)
                cols = slice(128 * t, 128 * t + 128)
                nc.tensor.matmul_mx(
                    out=acc[:],
                    lhsT=x_codes[:, g, cols].bitcast(FP8X4),
                    lhsT_scale=x_scales[:, g, cols],
                    rhs=c_codes[:, a].bitcast(FP8X4),
                    rhs_scale=c_scales[:, a],
                    start=True,
                    stop=True,
                )
                z[n].append(acc)

        def exp(n):
            tile = work.tile([P, R], F32, name="e_sb", bufs=3)
            for a in range(A):
                nc.scalar.activation(tile[:, 512 * a : 512 * a + 512], z[n][a][:], ACT.Exp)
            e_sb[n] = tile

        def strength(n):
            g, t = divmod(n, 4)
            if t == 0:
                tile = work.tile([P, 4, R], BF16, name="h_planes")
                h_planes[g] = tile
            nc.vector.scalar_tensor_tensor(
                out=h_planes[g][:, t, :], in0=e_sb[n][:], scalar=st[:, n : n + 1], in1=rule_b[:], op0=MULT, op1=MULT
            )

        def h_turn(n):
            g, t = divmod(n, 4)
            tr = bank([P, A, 2, P], "tr", 2)
            words = h_planes[g][:, t, :].bitcast(F32)
            for a in range(A):
                for u in range(2):
                    first = 256 * a + 128 * u
                    nc.tensor.transpose(tr[:, a, u, :], words[:, first : first + 128], ident[:])
            h_turned[n] = tr

        h_words = {}

        def h_copy(n):
            tile = work.tile([P, A, P, 2], F32, name="h_words", align_bytes=64, bufs=3)
            nc.scalar.copy(out=tile[:], in_=h_turned[n][:].rearrange("m a u p -> m a p u"))
            h_words[n] = tile

        def h_quant(n):
            codes = work.tile([P, A * P], U32, name="h_codes", align_bytes=64, bufs=3)
            scales = work.tile([P, A * P], U8, name="h_scales", align_bytes=64, bufs=3)
            quantize(codes[:], scales[:], h_words[n][:].rearrange("m a p u -> m (a p u)").bitcast(BF16))
            h_q[n] = (codes, scales)

        blend = {}
        out_view = out_0.rearrange("(g p t) n -> g t p n", p=P, t=4)

        def blend_mm(n):
            codes, scales = h_q[n]
            blend[n] = []
            for half in range(2):
                acc = bank([P, 512], "mm", 4)
                for a in range(A):
                    cols = slice(128 * a, 128 * a + 128)
                    nc.tensor.matmul_mx(
                        out=acc[:],
                        lhsT=codes[:, cols].bitcast(FP8X4),
                        lhsT_scale=scales[:, cols],
                        rhs=g_words[:, a, 1024 * half : 1024 * half + 1024].bitcast(FP4X4),
                        rhs_scale=g_scales[:, a, 512 * half : 512 * half + 512],
                        start=(a == 0),
                        stop=(a == A - 1),
                    )
                blend[n].append(acc)

        def blend_out(n, engines):
            g, t = divmod(n, 4)
            tile = work.tile([P, N], F32, name="blend_sb", bufs=4)
            for half in range(2):
                cols = slice(512 * half, 512 * half + 512)
                if engines[half] == "s":
                    nc.scalar.copy(out=tile[:, cols], in_=blend[n][half][:])
                else:
                    nc.vector.tensor_copy(out=tile[:, cols], in_=blend[n][half][:])
            nc.sync.dma_start(out=out_view[g, t], in_=tile[:])

        b_grouped = {}

        def b_group(g, parts, copy):
            if g not in b_grouped:
                tile = work.tile([P, A, 2, 2, P, 4], BF16, name="b_grouped", align_bytes=64)
                b_grouped[g] = tile
            for part in parts:
                a, u = divmod(part, 2)
                cols = slice(512 * a + 256 * u, 512 * a + 256 * u + 256)
                for e in range(2):
                    copy(
                        out=b_grouped[g][:, a, u, e].rearrange("p (c i) t -> p c t i", i=4),
                        in_=h_planes[g][:, :, cols].rearrange("p t (c i e) -> p e c t i", i=4, e=2)[:, e],
                    )

        def b_quant(g, a):
            cols = slice(512 * a, 512 * a + 512)
            quantize(b_codes[:, g, cols], b_scales[:, g, cols], b_grouped[g][:, a].rearrange("p u e m t -> p (u e m t)"))

        r_grouped = {}

        def r_group(g, half, copy):
            if g not in r_grouped:
                tile = work.tile([P, D, 4], BF16, name="r_grouped", align_bytes=64)
                r_grouped[g] = tile
            cols = slice(256 * half, 256 * half + 256)
            copy(
                out=r_grouped[g][:, cols].rearrange("p (c i) t -> p c t i", i=4),
                in_=r_raw[:, g, :, cols].rearrange("p t (c i) -> p c t i", i=4),
            )

        def r_quant(g):
            quantize(r_codes[:, g], r_scales[:, g], r_grouped[g][:].rearrange("p d t -> p (d t)"))

        credit = {}
        credit_view = out_1.rearrange("(a m f) d -> a f m d", m=P, f=4)

        def credit_mm(c, groups):
            if c not in credit:
                credit[c] = bank([P, D], *({0: ("cr", 2), 1: ("cr", 2), 4: ("tr", 2), 5: ("tr", 2)}.get(c, ("mm", 4))))
            for g in groups:
                cols = slice(128 * c, 128 * c + 128)
                nc.tensor.matmul_mx(
                    out=credit[c][:],
                    lhsT=b_codes[:, g, cols].bitcast(FP8X4),
                    lhsT_scale=b_scales[:, g, cols],
                    rhs=r_codes[:, g].bitcast(FP8X4),
                    rhs_scale=r_scales[:, g],
                    start=(g == 0),
                    stop=(g == G - 1),
                )

        def credit_out(c):
            tile = work.tile([P, D], F32, name="credit_sb", bufs=8)
            if c % 2:
                nc.scalar.copy(out=tile[:], in_=credit[c][:])
            else:
                nc.vector.tensor_copy(out=tile[:], in_=credit[c][:])
            nc.sync.dma_start(out=credit_view[c // 4, c % 4], in_=tile[:])

        vcopy, scopy = nc.vector.tensor_copy, nc.scalar.copy
        tr = bank([P, 4, P], "cr", 2)
        for f in range(4):
            nc.tensor.transpose(tr[:, f], x_col[:, f : f + 1].to_broadcast([P, P]), ident[:])
        scopy(out=x_sc[:], in_=tr[:].rearrange("p f m -> p m f"))
        x_widen(0, 0)
        x_widen(0, 1)
        for u in range(2):
            c_copy(0, u, c_turn(0, u), scopy)
        tr = x_turn(0, 0)
        c_quant(0, 0)
        c_quant(0, 1)
        x_copy(0, 0, tr)
        tr = x_turn(0, 1)
        x_quant(0, ((0, 1),))
        for u in range(2):
            c_copy(1, u, c_turn(1, u), scopy)
        x_widen(1, 0)
        for a, copy in ((0, vcopy), (1, scopy)):
            acc = bank([P, 512], "cr", 2)
            nc.tensor.matmul(
                acc[:].rearrange("p (u m e) -> p u m e", u=2, e=2),
                lhsT=ones[:],
                rhs=rule_row[:, 512 * a : 512 * a + 512].rearrange("k (m u e) -> k u m e", u=2, e=2),
                start=True,
                stop=True,
            )
            copy(out=rule_b[:, 512 * a : 512 * a + 512], in_=acc[:])
        c_quant(1, 0)
        c_quant(1, 1)
        x_copy(0, 1, tr)
        z_mm(0)
        exp(0)
        x_quant(0, ((1, 1),))
        z_mm(1)
        exp(1)
        tr = x_turn(1, 0)
        z_mm(2)
        x_widen(1, 1)
        strength(0)
        x_copy(1, 0, tr)

        widen = {2: (2, 0), 3: (2, 1), 5: (3, 0), 6: (3, 1)}
        turn = {0: (1, 1), 3: (2, 0), 4: (2, 1), 6: (3, 0), 7: (3, 1)}
        quant = {1: 1, 5: 2, 8: 3}
        r_groups = {1: [(0, 0), (0, 1)], 9: [(1, 0), (1, 1)]}
        r_quants = {2: 0, 10: 1}
        b_vector = {3: [(0, 0), (0, 1)], 4: [(0, 2)], 5: [(0, 3)], 7: [(1, 0), (1, 1)], 8: [(1, 2)], 9: [(1, 3)], 11: [(2, 0), (2, 1)], 12: [(2, 2), (2, 3)],}
        b_scalar = {}
        b_quants = {5: [(0, 0)], 6: [(0, 1)], 9: [(1, 0)], 10: [(1, 1)], 13: [(2, 0), (2, 1)]}
        early = {7: [(0, 0), (1, 0)], 11: [(0, 1), (1, 1)], 13: [(2, 0), (2, 1), (3, 0), (3, 1)]}
        for s in range(TILES - 2):
            h_turn(s)
            turned = x_turn(*turn[s]) if s in turn else None
            if s + 2 < TILES:
                exp(s + 2)
            h_copy(s)
            if turned is not None:
                x_copy(*turn[s], turned)
            strength(s + 1)
            if s >= 1:
                h_quant(s - 1)
            for g, part in b_scalar.get(s, []):
                b_group(g, [part], scopy)
            if s in quant:
                x_quant(quant[s], ((0, 2),))
            if s in widen:
                x_widen(*widen[s])
            for g, half in r_groups.get(s, []):
                r_group(g, half, scopy if half else vcopy)
            for g, part in b_vector.get(s, []):
                b_group(g, [part], vcopy)
            for g, a in b_quants.get(s, []):
                b_quant(g, a)
            if s in r_quants:
                r_quant(r_quants[s])
            if 2 <= s:
                blend_mm(s - 2)
                blend_out(s - 2, "ss")
            if s + 3 < TILES:
                z_mm(s + 3)
            for c, g in early.get(s, []):
                credit_mm(c, [g])
        n = TILES - 2
        h_turn(n)
        h_copy(n)
        strength(n + 1)
        h_quant(n - 1)
        blend_mm(n - 2)
        blend_out(n - 2, "ss")
        h_turn(n + 1)
        r_group(2, 0, vcopy)
        h_copy(n + 1)
        r_group(2, 1, scopy)
        h_quant(n)
        b_group(3, [0, 1], vcopy)
        r_quant(2)
        blend_mm(n - 1)
        blend_out(n - 1, "ss")
        h_quant(n + 1)
        for c in (4, 5):
            credit_mm(c, range(2))
        b_group(3, [2, 3], vcopy)
        r_group(3, 1, scopy)
        r_group(3, 0, vcopy)
        blend_mm(n)
        blend_out(n, "ss")
        b_quant(3, 0)
        r_quant(3)
        b_quant(3, 1)
        for c in range(6):
            credit_mm(c, [2])
        blend_mm(n + 1)
        blend_out(n + 1, "sv")
        for c in range(6):
            credit_mm(c, [3])
            credit_out(c)
        credit_mm(6, range(4))
        credit_out(6)
        credit_mm(7, range(4))
        for half, copy in ((0, scopy), (1, vcopy)):
            cols = slice(256 * half, 256 * half + 256)
            tile = work.tile([P, 256], F32, name="credit_half", bufs=2)
            copy(out=tile[:], in_=credit[7][:, cols])
            nc.sync.dma_start(out=credit_view[1, 3][:, cols], in_=tile[:])
